import numpy as np
import ml_dtypes


def mxq(x, axis, fmt="e4m3"):
    dtype, down = {"e4m3": (ml_dtypes.float8_e4m3fn, 7), "e5m2": (ml_dtypes.float8_e5m2, 14)}[fmt]
    v = np.moveaxis(np.asarray(x, np.float32).astype(ml_dtypes.bfloat16).astype(np.float64), axis, -1)
    blocks = v.reshape(v.shape[:-1] + (-1, 32))
    amax = np.abs(blocks).max(-1, keepdims=True)
    byte = np.maximum(np.where(amax > 0, np.frexp(amax)[1] - 1 + 127, 0) - down, 1)
    scale = np.exp2(byte - 127.0)
    codes = (blocks / scale).astype(np.float32).astype(dtype).astype(np.float64)
    return np.moveaxis((codes * scale).reshape(v.shape), -1, axis)


WIDE = False


def mx_kscale(k):
    if not WIDE:
        return np.ones(k)
    levels = np.array([10, -10, 5, -5, 0])
    if k % 512:
        return np.exp2(np.random.permutation(np.resize(levels, k // 32))).repeat(32)
    a = np.empty((k // 512, 16))
    for p in range(k // 512):
        a[p, :8] = np.random.permutation(np.resize(levels, 8))
        for g in range(8):
            far = levels[np.abs(levels - a[p, g]) >= 10]
            a[p, g + 8] = far[np.random.randint(len(far))]
    return np.exp2(a.ravel()).repeat(32)


def f64(x):
    return np.asarray(x).astype(np.float64)


def striped(idx):
    return np.tile(np.asarray(idx).reshape(-1, 16).T, (8, 1)).astype(np.uint16)


def unstriped(offs):
    return offs[:16].T.reshape(-1).astype(np.int64)


E2M1 = np.array([0.0, 0.5, 1.0, 1.5, 2.0, 3.0, 4.0, 6.0, -0.0, -0.5, -1.0, -1.5, -2.0, -3.0, -4.0, -6.0])


def pack_weight(w, fmt):
    k, n = w.shape
    w = f64(np.asarray(w, np.float32).astype(ml_dtypes.bfloat16)).reshape(k // 32, 32, n)
    amax = np.abs(w).max(1)
    if fmt == "e4m3":
        byte = np.frexp(amax)[1] - 1 + 127 - 7
    else:
        mant, ex = np.frexp(amax / 6.0)
        byte = np.where(mant > 0.5, ex, ex - 1) + 127
    byte = np.clip(np.where(amax > 0, byte, 1), 1, 254)
    scaled = (w * np.exp2(127.0 - byte)[:, None, :]).reshape(k, n).astype(np.float32)
    by_word = np.ascontiguousarray(scaled.reshape(k // 512, 128, 4, n).transpose(0, 1, 3, 2))
    if fmt == "e4m3":
        words = by_word.astype(ml_dtypes.float8_e4m3fn).view(np.uint8)
    else:
        c = by_word.astype(ml_dtypes.float4_e2m1fn).view(np.uint8) & 0xF
        words = (c[..., 0::2] | (c[..., 1::2] << 4)).reshape(k // 512, 128, 2 * n)
    return np.ascontiguousarray(words), np.ascontiguousarray(byte.astype(np.uint8).reshape(k // 512, 16, n))


def unpack_weight(words, scales, fmt):
    g, _, n = scales.shape
    words = np.ascontiguousarray(words).reshape(g, 128, n, -1)
    if fmt == "e4m3":
        vals = words.view(ml_dtypes.float8_e4m3fn).astype(np.float64)
    else:
        nib = np.empty((g, 128, n, 4), np.uint8)
        nib[..., 0::2] = words & 0xF
        nib[..., 1::2] = words >> 4
        vals = E2M1[nib]
    vals = vals * np.repeat(np.exp2(scales.astype(np.float64) - 127.0), 8, axis=1)[..., None]
    return vals.transpose(0, 1, 3, 2).reshape(g * 512, n)


def bf(x):
    return np.asarray(x, np.float32).astype(ml_dtypes.bfloat16)


def planes(Y):
    r, m = Y.shape
    b = f64(bf(Y)).reshape(r // 32, 32, m)
    amax = np.abs(b).max(1)
    byte = np.clip(np.where(amax > 0, np.frexp(amax)[1] - 1 + 127 - 7, 1), 1, 254)
    codes = (b * np.exp2(127.0 - byte)[:, None, :]).reshape(r, m).astype(np.float32).astype(ml_dtypes.float8_e4m3fn).view(np.uint8)
    words = codes.reshape(r // 512, 128, 4, m).transpose(0, 1, 3, 2)
    return np.ascontiguousarray(words), np.ascontiguousarray(byte.astype(np.uint8).reshape(r // 512, 16, m))


D, T, I, Q, E, K = 512, 2048, 512, 256, 512, 512


def setup_inputs():
    n = np.random.standard_normal
    idx = np.random.permutation(T)[:I]
    fd = mx_kscale(D)
    fk = mx_kscale(K)
    fi = mx_kscale(I)
    ti = np.ones(T)
    ti[idx] = fi
    keysp = pack_weight(n((D, T)) / fd[:, None], "e2m1")
    return {
        "query": (n((D, Q)) * 0.4 / np.sqrt(D) * fd[:, None]).astype(np.float32),
        "query2": (n((K, Q)) * 0.4 / np.sqrt(K) * fk[:, None]).astype(np.float32),
        "keys_words": keysp[0],
        "keys_scales": keysp[1],
        "keys2": (n((K, T)) / fk[:, None]).astype(np.float32),
        "l1": (np.random.uniform(6.2, 6.5, (Q, 1))).astype(np.float32),
        "l2": (np.random.uniform(6.4, 6.7, (Q, 1))).astype(np.float32),
        "size": (np.random.uniform(0.02, 0.08, (1, I)) * fi).astype(np.float32),
        "vals": (n((E, T)) / ti).astype(np.float32),
        "offs": striped(idx),
    }


def reference(query, query2, keys_words, keys_scales, keys2, l1, l2, size, vals, offs):
    idx = unstriped(offs)
    keysu = unpack_weight(keys_words, keys_scales, "e2m1")
    queryq = mxq(f64(query), 0, "e4m3")
    keysidxg = keysu[:, idx]
    a = queryq.T @ keysidxg
    query2q = mxq(f64(query2), 0, "e4m3")
    keys2idxq = mxq(f64(keys2)[:, idx], 0, "e4m3")
    b = query2q.T @ keys2idxq
    r = np.minimum(np.exp(a - f64(l1) - b + f64(l2)), 2.0) * f64(size)
    wt = r.T
    vt = f64(vals)[:, idx].T
    vtq = mxq(vt, 0, "e4m3")
    wtq = mxq(wt, 0, "e4m3")
    o = vtq.T @ wtq
    words, scales = planes(o)
    return o, words, scales

@@ -1,0 +1,204 @@
+from contextlib import ExitStack
+
+import concourse.mybir as mybir
+from concourse.masks import make_identity
+
+F32 = mybir.dt.float32
+BF16 = mybir.dt.bfloat16
+I32 = mybir.dt.int32
+U32 = mybir.dt.uint32
+U16 = mybir.dt.uint16
+U8 = mybir.dt.uint8
+FP8X4 = mybir.dt.float8_e4m3fn_x4
+FP4X4 = mybir.dt.float4_e2m1fn_x4
+ALU = mybir.AluOpType
+ACT = mybir.ActivationFunctionType
+
+D, T, I, Q, E, K = 512, 2048, 512, 256, 512, 512
+P = 128
+PACK = 4
+HALVES = Q // P
+FLOPS = 2 * Q * I * (D + K + E)
+
+
+def tile_attend_importanceread_pl_kernel(
+    tc, query, query2, keys_words, keys_scales, keys2, l1, l2, size, vals, offs, out_0, out_1, out_2
+):
+    nc = tc.nc
+    with ExitStack() as ctx:
+        keep = ctx.enter_context(tc.tile_pool(name="keep", bufs=1))
+        psum = ctx.enter_context(tc.psum_pool(name="psum", bufs=1))
+        psum2 = ctx.enter_context(tc.psum_pool(name="psum2", bufs=2))
+
+        def sb(name, shape, dtype, tag=None):
+            return keep.tile(shape, dtype, name=name, tag=tag or name, align_bytes=64)
+
+        def quantize(codes, scales, grouped):
+            nc.vector.quantize_mx(out=codes.bitcast(FP8X4), scales=scales, in_=grouped)
+
+        kscale_pool = sb("kscale_pool", [P, T], U8)
+        nc.gpsimd.memset(kscale_pool[:].bitcast(I32), 0)
+
+        keys2_planes = keys2.rearrange("(p t) n -> t p n", t=PACK)
+        vals_planes = vals.rearrange("(p t) n -> t p n", t=PACK)
+        k2_pool = [sb("k2_pool%d" % t, [P, T], F32) for t in range(PACK)]
+        v_pool = [sb("v_pool%d" % t, [P, T], F32) for t in range(PACK)]
+        offsets = keep.tile([P, I // 16], U16, name="offsets")
+        l1_sb = sb("l1_sb", [P, HALVES], F32)
+        l2_sb = sb("l2_sb", [P, HALVES], F32)
+        size_sb = sb("size_sb", [P, PACK], F32)
+        kword_pool = sb("kword_pool", [P, T], U16)
+        q_raw = sb("q_raw", [P, PACK, Q], F32)
+        q2_raw = sb("q2_raw", [P, PACK, Q], F32)
+        nc.sync.dma_start(k2_pool[0][:], keys2_planes[0])
+        nc.sync.dma_start(offsets[:], offs)
+        with nc.allow_non_contiguous_dma(reason="one value a partition and half"):
+            nc.sync.dma_start(l1_sb[:], l1.rearrange("(h p) o -> p (h o)", p=P))
+            nc.sync.dma_start(l2_sb[:], l2.rearrange("(h p) o -> p (h o)", p=P))
+        nc.sync.dma_start(size_sb[:], size.rearrange("o (p t) -> p (o t)", t=PACK))
+        nc.sync.dma_start(k2_pool[1][:], keys2_planes[1])
+        for g in range(4):
+            nc.sync.dma_start(
+                kscale_pool[32 * g : 32 * g + 4, :].bitcast(I32), keys_scales[0, 4 * g : 4 * g + 4, :].bitcast(I32)
+            )
+        nc.sync.dma_start(q2_raw[:], query2.rearrange("(p t) q -> p t q", t=PACK))
+        for t in range(2, PACK):
+            nc.sync.dma_start(k2_pool[t][:], keys2_planes[t])
+        nc.sync.dma_start(q_raw[:], query.rearrange("(p t) q -> p t q", t=PACK))
+        nc.sync.dma_start(kword_pool[:].bitcast(I32), keys_words[0].bitcast(I32))
+        for t in range(PACK):
+            nc.sync.dma_start(v_pool[t][:], vals_planes[t])
+
+        ident = sb("ident", [P, P], F32)
+        make_identity(nc, ident[:])
+
+        k2_grp = sb("k2_grp", [P, I, PACK], BF16)
+        kscale = sb("kscale", [P, I], U8)
+        kword = sb("kword", [P, I], U16)
+        nc.vector.tensor_copy(k2_grp[:, :, 0], k2_pool[0][:].indirect(offsets[:]))
+        nc.vector.tensor_copy(k2_grp[:, :, 1], k2_pool[1][:].indirect(offsets[:]))
+        nc.vector.tensor_copy(kscale[:], kscale_pool[:].indirect(offsets[:]))
+        for t in range(2, PACK):
+            nc.vector.tensor_copy(k2_grp[:, :, t], k2_pool[t][:].indirect(offsets[:]))
+
+        nc.vector.tensor_copy(kword[:], kword_pool[:].indirect(offsets[:]))
+        bias = sb("bias", [P, HALVES], F32)
+        nc.vector.tensor_tensor(bias[:], l2_sb[:], l1_sb[:], ALU.subtract)
+
+        q_grp = sb("q_grp", [P, Q, PACK], BF16)
+        q2_grp = sb("q2_grp", [P, Q, PACK], BF16)
+        nc.scalar.copy(
+            q_grp[:].rearrange("p (c i) t -> p c t i", i=4), q_raw[:].rearrange("p t (c i) -> p c t i", i=4)
+        )
+        nc.vector.tensor_scalar(
+            q2_grp[:].rearrange("p (c i) t -> p c t i", i=4),
+            q2_raw[:].rearrange("p t (c i) -> p c t i", i=4),
+            -1.0,
+            None,
+            ALU.mult,
+        )
+        q_codes, q_scales = sb("q_codes", [P, Q], U32), sb("q_scales", [P, Q], U8)
+        q2_codes, q2_scales = sb("q2_codes", [P, Q], U32), sb("q2_scales", [P, Q], U8)
+        k2_codes, k2_scales = sb("k2_codes", [P, I], U32), sb("k2_scales", [P, I], U8)
+        quantize(k2_codes[:], k2_scales[:], k2_grp[:].rearrange("p i t -> p (i t)"))
+        quantize(q2_codes[:], q2_scales[:], q2_grp[:].rearrange("p q t -> p (q t)"))
+        quantize(q_codes[:], q_scales[:], q_grp[:].rearrange("p q t -> p (q t)"))
+
+        ratio_t = []
+        for h in range(HALVES):
+            cols = slice(h * P, (h + 1) * P)
+            score = psum.tile([P, I], F32, name="score%d" % h)
+            nc.tensor.matmul_mx(
+                out=score[:], lhsT=q2_codes[:, cols].bitcast(FP8X4), lhsT_scale=q2_scales[:, cols],
+                rhs=k2_codes[:].bitcast(FP8X4), rhs_scale=k2_scales[:], start=True, stop=False,
+            )
+            nc.tensor.matmul_mx(
+                out=score[:], lhsT=q_codes[:, cols].bitcast(FP8X4), lhsT_scale=q_scales[:, cols],
+                rhs=kword[:].bitcast(FP4X4), rhs_scale=kscale[:], start=False, stop=True,
+            )
+            ratio = sb("ratio%d" % h, [P, PACK, P], F32)
+            nc.scalar.activation(
+                ratio[:], score[:].rearrange("p (s t) -> p t s", t=PACK), ACT.Exp, bias=bias[:, h : h + 1]
+            )
+            ratio_t.append(psum.tile([P, PACK, P], F32, name="ratio_t%d" % h))
+            for t in range(PACK):
+                nc.tensor.transpose(ratio_t[h][:, t, :], ratio[:, t, :], ident[:])
+
+        out_rows = out_0.rearrange("(p t) q -> p t q", t=PACK)
+        acc = [psum.tile([P, PACK, P], F32, name="acc%d" % h) for h in range(HALVES)]
+        o_grp = sb("o_grp", [P, Q, PACK], BF16)
+        v_grp01 = sb("v_grp01", [P, 2 * P * PACK], BF16)
+        v_grp2 = sb("v_grp2", [P, P * PACK], BF16)
+        v_grp3 = sb("v_grp3", [P, P * PACK], BF16)
+        v_grp = [v_grp01[:, : P * PACK], v_grp01[:, P * PACK :], v_grp2[:], v_grp3[:]]
+        v_scales = sb("v_scales", [P, PACK, P], U8)
+
+        def turn(t):
+            v_g = sb("v_g%d" % t, [P, I], BF16)
+            nc.vector.tensor_copy(v_g[:], v_pool[t][:].indirect(offsets[:]))
+            words = v_g[:].bitcast(F32)
+            v_t = psum2.tile([P, 2, P], F32, name="v_t")
+            for u in range(2):
+                nc.tensor.transpose(v_t[:, u, :], words[:, u : 2 * P : 2], ident[:])
+            nc.scalar.copy(
+                v_grp[t].bitcast(F32).rearrange("p (e u) -> p e u", u=2), v_t[:].rearrange("p u e -> p e u")
+            )
+
+        def quantize_values(grouped, t0, t1, tag):
+            v_codes = sb("v_codes%d" % t0, [P, t1 - t0, P], U32, tag)
+            quantize(
+                v_codes[:].rearrange("p t e -> p (t e)"),
+                v_scales[:, t0:t1, :].rearrange("p t e -> p (t e)"),
+                grouped,
+            )
+            return v_codes
+
+        def multiply(v_codes, t0, t1):
+            for t in range(t0, t1):
+                for h in range(HALVES):
+                    cols = slice(h * P, (h + 1) * P)
+                    nc.tensor.matmul_mx(
+                        out=acc[h][:, t, :], lhsT=v_codes[:, t - t0, :].bitcast(FP8X4), lhsT_scale=v_scales[:, t, :],
+                        rhs=w_codes[:, cols].bitcast(FP8X4), rhs_scale=w_scales[:, cols], start=True, stop=True,
+                    )
+
+        def store(t0, t1):
+            o_sb = sb("o_sb%d" % t0, [P, t1 - t0, Q], F32)
+            for h in reversed(range(HALVES)):
+                nc.scalar.copy(o_sb[:, :, h * P : (h + 1) * P], acc[h][:, t0:t1, :])
+            nc.sync.dma_start(out_rows[:, t0:t1, :], o_sb[:])
+
+        turn(0)
+        turn(1)
+        w_grp = sb("w_grp", [P, Q, PACK], BF16, "v_pool1")
+        for h in range(HALVES):
+            nc.vector.scalar_tensor_tensor(
+                w_grp[:, h * P : (h + 1) * P, :],
+                ratio_t[h][:].rearrange("p t q -> p q t"),
+                2.0,
+                size_sb[:].unsqueeze(1).broadcast_to([P, P, PACK]),
+                ALU.min,
+                ALU.mult,
+            )
+        codes01 = quantize_values(v_grp01[:], 0, 2, None)
+        turn(2)
+        w_codes, w_scales = sb("w_codes", [P, Q], U32, "v_pool2"), sb("w_scales", [P, Q], U8)
+        quantize(w_codes[:], w_scales[:], w_grp[:].rearrange("p q t -> p (q t)"))
+        multiply(codes01, 0, 2)
+        store(0, 2)
+        turn(3)
+        multiply(quantize_values(v_grp2[:], 2, 3, "v_pool3"), 2, 3)
+        store(2, 3)
+        multiply(quantize_values(v_grp3[:], 3, 4, None), 3, 4)
+        nc.vector.tensor_copy(o_grp[:, 0:P, :], acc[0][:].rearrange("p t q -> p q t"))
+        nc.scalar.copy(o_grp[:, P:Q, :], acc[1][:].rearrange("p t q -> p q t"))
+        store(PACK - 1, PACK)
+
+        o_codes, o_scales = sb("o_codes", [P, Q], U32), sb("o_scales", [P, Q], U8)
+        quantize(o_codes[:], o_scales[:], o_grp[:].rearrange("p q t -> p (q t)"))
+        nc.sync.dma_start(out_1[0].rearrange("p c r -> p (c r)").bitcast(I32), o_codes[:].bitcast(I32))
+        for g in range(4):
+            eng = nc.scalar if g % 2 == 0 else nc.sync
+            eng.dma_start(
+                out_2[0, 4 * g : 4 * g + 4, :].bitcast(I32), o_scales[32 * g : 32 * g + 4, :].bitcast(I32)
+            )

@@ -44,64 +44,72 @@ def tile_attend_importanceread_pl_kernel(
         k2_pool = [sb("k2_pool%d" % t, [P, T], F32) for t in range(PACK)]
         v_pool = [sb("v_pool%d" % t, [P, T], F32) for t in range(PACK)]
         offsets = keep.tile([P, I // 16], U16, name="offsets")
-        l1_sb = sb("l1_sb", [P, HALVES], F32)
-        l2_sb = sb("l2_sb", [P, HALVES], F32)
-        size_sb = sb("size_sb", [P, PACK], F32)
+        rows = sb("rows", [P, I + P], F32)
+        nc.vector.memset(rows[:], 0.0)
         kword_pool = sb("kword_pool", [P, T], U16)
         q_raw = sb("q_raw", [P, PACK, Q], F32)
         q2_raw = sb("q2_raw", [P, PACK, Q], F32)
         nc.sync.dma_start(k2_pool[0][:], keys2_planes[0])
         nc.sync.dma_start(offsets[:], offs)
-        with nc.allow_non_contiguous_dma(reason="one value a partition and half"):
-            nc.sync.dma_start(l1_sb[:], l1.rearrange("(h p) o -> p (h o)", p=P))
-            nc.sync.dma_start(l2_sb[:], l2.rearrange("(h p) o -> p (h o)", p=P))
-        nc.sync.dma_start(size_sb[:], size.rearrange("o (p t) -> p (o t)", t=PACK))
         nc.sync.dma_start(k2_pool[1][:], keys2_planes[1])
         for g in range(4):
             nc.sync.dma_start(
-                kscale_pool[32 * g : 32 * g + 4, :].bitcast(I32), keys_scales[0, 4 * g : 4 * g + 4, :].bitcast(I32)
+                kscale_pool[g:P:32, :].bitcast(I32), keys_scales[0, g:16:4, :].bitcast(I32)
             )
-        nc.sync.dma_start(q2_raw[:], query2.rearrange("(p t) q -> p t q", t=PACK))
         for t in range(2, PACK):
             nc.sync.dma_start(k2_pool[t][:], keys2_planes[t])
+        nc.sync.dma_start(q2_raw[:], query2.rearrange("(p t) q -> p t q", t=PACK))
         nc.sync.dma_start(q_raw[:], query.rearrange("(p t) q -> p t q", t=PACK))
         nc.sync.dma_start(kword_pool[:].bitcast(I32), keys_words[0].bitcast(I32))
         for t in range(PACK):
             nc.sync.dma_start(v_pool[t][:], vals_planes[t])
+        nc.gpsimd.dma_start(rows[0:HALVES, I:], l1.rearrange("(h p) o -> h (p o)", p=P))
+        nc.gpsimd.dma_start(rows[HALVES : 2 * HALVES, I:], l2.rearrange("(h p) o -> h (p o)", p=P))
+        nc.gpsimd.dma_start(rows[0:1, :I], size)
 
         ident = sb("ident", [P, P], F32)
         make_identity(nc, ident[:])
 
+        size_t = psum.tile([P, PACK, P], F32, name="size_t", tag="acc0")
+        for t in range(PACK):
+            nc.tensor.transpose(size_t[:, t, :], rows[:, t:I:PACK], ident[:])
+        size_sb = sb("size_sb", [P, PACK], F32)
+        nc.scalar.copy(size_sb[:], size_t[:, :, 0])
+        l_t = psum.tile([P, P], F32, name="l_t", tag="acc1")
+        nc.tensor.transpose(l_t[:], rows[:, I:], ident[:])
+        l_sb = sb("l_sb", [P, 2 * HALVES], F32)
+        nc.scalar.copy(l_sb[:], l_t[:, : 2 * HALVES])
+
+        k2_g = sb("k2_g", [P, 2, I], BF16)
         k2_grp = sb("k2_grp", [P, I, PACK], BF16)
         kscale = sb("kscale", [P, I], U8)
         kword = sb("kword", [P, I], U16)
-        nc.vector.tensor_copy(k2_grp[:, :, 0], k2_pool[0][:].indirect(offsets[:]))
-        nc.vector.tensor_copy(k2_grp[:, :, 1], k2_pool[1][:].indirect(offsets[:]))
+        nc.vector.tensor_copy(k2_g[:, 0, :], k2_pool[0][:].indirect(offsets[:]))
+        nc.vector.tensor_copy(k2_g[:, 1, :], k2_pool[1][:].indirect(offsets[:]))
         nc.vector.tensor_copy(kscale[:], kscale_pool[:].indirect(offsets[:]))
+        nc.scalar.copy(k2_grp[:, :, 0:2], k2_g[:].rearrange("p t i -> p i t"))
         for t in range(2, PACK):
             nc.vector.tensor_copy(k2_grp[:, :, t], k2_pool[t][:].indirect(offsets[:]))
-
-        nc.vector.tensor_copy(kword[:], kword_pool[:].indirect(offsets[:]))
         bias = sb("bias", [P, HALVES], F32)
-        nc.vector.tensor_tensor(bias[:], l2_sb[:], l1_sb[:], ALU.subtract)
+        nc.vector.tensor_tensor(bias[:], l_sb[:, HALVES:], l_sb[:, :HALVES], ALU.subtract)
 
         q_grp = sb("q_grp", [P, Q, PACK], BF16)
         q2_grp = sb("q2_grp", [P, Q, PACK], BF16)
-        nc.scalar.copy(
-            q_grp[:].rearrange("p (c i) t -> p c t i", i=4), q_raw[:].rearrange("p t (c i) -> p c t i", i=4)
-        )
-        nc.vector.tensor_scalar(
+        nc.scalar.activation(
             q2_grp[:].rearrange("p (c i) t -> p c t i", i=4),
             q2_raw[:].rearrange("p t (c i) -> p c t i", i=4),
-            -1.0,
-            None,
-            ALU.mult,
+            ACT.Copy,
+            scale=-1.0,
+        )
+        nc.scalar.copy(
+            q_grp[:].rearrange("p (c i) t -> p c t i", i=4), q_raw[:].rearrange("p t (c i) -> p c t i", i=4)
         )
         q_codes, q_scales = sb("q_codes", [P, Q], U32), sb("q_scales", [P, Q], U8)
         q2_codes, q2_scales = sb("q2_codes", [P, Q], U32), sb("q2_scales", [P, Q], U8)
         k2_codes, k2_scales = sb("k2_codes", [P, I], U32), sb("k2_scales", [P, I], U8)
         quantize(k2_codes[:], k2_scales[:], k2_grp[:].rearrange("p i t -> p (i t)"))
         quantize(q2_codes[:], q2_scales[:], q2_grp[:].rearrange("p q t -> p (q t)"))
+        nc.vector.tensor_copy(kword[:], kword_pool[:].indirect(offsets[:]))
         quantize(q_codes[:], q_scales[:], q_grp[:].rearrange("p q t -> p (q t)"))
 
         ratio_t = []
@@ -125,13 +133,9 @@ def tile_attend_importanceread_pl_kernel(
                 nc.tensor.transpose(ratio_t[h][:, t, :], ratio[:, t, :], ident[:])
 
         out_rows = out_0.rearrange("(p t) q -> p t q", t=PACK)
-        acc = [psum.tile([P, PACK, P], F32, name="acc%d" % h) for h in range(HALVES)]
+        acc = [psum.tile([P, PACK, P], F32, name="acc%d" % h, tag="acc%d" % h) for h in range(HALVES)]
         o_grp = sb("o_grp", [P, Q, PACK], BF16)
-        v_grp01 = sb("v_grp01", [P, 2 * P * PACK], BF16)
-        v_grp2 = sb("v_grp2", [P, P * PACK], BF16)
-        v_grp3 = sb("v_grp3", [P, P * PACK], BF16)
-        v_grp = [v_grp01[:, : P * PACK], v_grp01[:, P * PACK :], v_grp2[:], v_grp3[:]]
-        v_scales = sb("v_scales", [P, PACK, P], U8)
+        PLANE = P * PACK
 
         def turn(t):
             v_g = sb("v_g%d" % t, [P, I], BF16)
@@ -140,27 +144,20 @@ def tile_attend_importanceread_pl_kernel(
             v_t = psum2.tile([P, 2, P], F32, name="v_t")
             for u in range(2):
                 nc.tensor.transpose(v_t[:, u, :], words[:, u : 2 * P : 2], ident[:])
+            return v_t
+
+        def group(v_t, grouped):
             nc.scalar.copy(
-                v_grp[t].bitcast(F32).rearrange("p (e u) -> p e u", u=2), v_t[:].rearrange("p u e -> p e u")
+                grouped.bitcast(F32).rearrange("p (e u) -> p e u", u=2), v_t[:].rearrange("p u e -> p e u")
             )
 
-        def quantize_values(grouped, t0, t1, tag):
-            v_codes = sb("v_codes%d" % t0, [P, t1 - t0, P], U32, tag)
-            quantize(
-                v_codes[:].rearrange("p t e -> p (t e)"),
-                v_scales[:, t0:t1, :].rearrange("p t e -> p (t e)"),
-                grouped,
-            )
-            return v_codes
-
-        def multiply(v_codes, t0, t1):
-            for t in range(t0, t1):
-                for h in range(HALVES):
-                    cols = slice(h * P, (h + 1) * P)
-                    nc.tensor.matmul_mx(
-                        out=acc[h][:, t, :], lhsT=v_codes[:, t - t0, :].bitcast(FP8X4), lhsT_scale=v_scales[:, t, :],
-                        rhs=w_codes[:, cols].bitcast(FP8X4), rhs_scale=w_scales[:, cols], start=True, stop=True,
-                    )
+        def multiply(t, v_codes, v_scales):
+            for h in range(HALVES):
+                cols = slice(h * P, (h + 1) * P)
+                nc.tensor.matmul_mx(
+                    out=acc[h][:, t, :], lhsT=v_codes.bitcast(FP8X4), lhsT_scale=v_scales,
+                    rhs=wv_codes[:, cols].bitcast(FP8X4), rhs_scale=wv_scales[:, cols], start=True, stop=True,
+                )
 
         def store(t0, t1):
             o_sb = sb("o_sb%d" % t0, [P, t1 - t0, Q], F32)
@@ -168,28 +165,36 @@ def tile_attend_importanceread_pl_kernel(
                 nc.scalar.copy(o_sb[:, :, h * P : (h + 1) * P], acc[h][:, t0:t1, :])
             nc.sync.dma_start(out_rows[:, t0:t1, :], o_sb[:])
 
-        turn(0)
-        turn(1)
-        w_grp = sb("w_grp", [P, Q, PACK], BF16, "v_pool1")
+        v_t0 = turn(0)
+        v_t1 = turn(1)
+        wv_grp = sb("wv_grp", [P, Q * PACK + 2 * PLANE], BF16, "v_pool1")
         for h in range(HALVES):
             nc.vector.scalar_tensor_tensor(
-                w_grp[:, h * P : (h + 1) * P, :],
+                wv_grp[:, h * PLANE : (h + 1) * PLANE].rearrange("p (q t) -> p q t", t=PACK),
                 ratio_t[h][:].rearrange("p t q -> p q t"),
                 2.0,
                 size_sb[:].unsqueeze(1).broadcast_to([P, P, PACK]),
                 ALU.min,
                 ALU.mult,
             )
-        codes01 = quantize_values(v_grp01[:], 0, 2, None)
-        turn(2)
-        w_codes, w_scales = sb("w_codes", [P, Q], U32, "v_pool2"), sb("w_scales", [P, Q], U8)
-        quantize(w_codes[:], w_scales[:], w_grp[:].rearrange("p q t -> p (q t)"))
-        multiply(codes01, 0, 2)
+        group(v_t0, wv_grp[:, 2 * PLANE : 3 * PLANE])
+        group(v_t1, wv_grp[:, 3 * PLANE : 4 * PLANE])
+        v_grp2 = sb("v_grp2", [P, PLANE], BF16)
+        group(turn(2), v_grp2[:])
+        wv_codes, wv_scales = sb("wv_codes", [P, 4 * P], U32, "v_pool2"), sb("wv_scales", [P, 4 * P], U8)
+        quantize(wv_codes[:], wv_scales[:], wv_grp[:])
+        for t in range(2):
+            multiply(t, wv_codes[:, Q + t * P : Q + (t + 1) * P], wv_scales[:, Q + t * P : Q + (t + 1) * P])
         store(0, 2)
-        turn(3)
-        multiply(quantize_values(v_grp2[:], 2, 3, "v_pool3"), 2, 3)
+        v_grp3 = sb("v_grp3", [P, PLANE], BF16)
+        group(turn(3), v_grp3[:])
+        v_codes2, v_scales2 = sb("v_codes2", [P, P], U32, "v_pool3"), sb("v_scales2", [P, P], U8)
+        quantize(v_codes2[:], v_scales2[:], v_grp2[:])
+        multiply(2, v_codes2[:], v_scales2[:])
         store(2, 3)
-        multiply(quantize_values(v_grp3[:], 3, 4, None), 3, 4)
+        v_codes3, v_scales3 = sb("v_codes3", [P, P], U32), sb("v_scales3", [P, P], U8)
+        quantize(v_codes3[:], v_scales3[:], v_grp3[:])
+        multiply(3, v_codes3[:], v_scales3[:])
         nc.vector.tensor_copy(o_grp[:, 0:P, :], acc[0][:].rearrange("p t q -> p q t"))
         nc.scalar.copy(o_grp[:, P:Q, :], acc[1][:].rearrange("p t q -> p q t"))
         store(PACK - 1, PACK)
@@ -200,5 +205,5 @@ def tile_attend_importanceread_pl_kernel(
         for g in range(4):
             eng = nc.scalar if g % 2 == 0 else nc.sync
             eng.dma_start(
-                out_2[0, 4 * g : 4 * g + 4, :].bitcast(I32), o_scales[32 * g : 32 * g + 4, :].bitcast(I32)
+                out_2[0, g:16:4, :].bitcast(I32), o_scales[g:P:32, :].bitcast(I32)
             )

from contextlib import ExitStack

import concourse.mybir as mybir
from concourse.masks import make_identity

F32 = mybir.dt.float32
BF16 = mybir.dt.bfloat16
I32 = mybir.dt.int32
U32 = mybir.dt.uint32
U16 = mybir.dt.uint16
U8 = mybir.dt.uint8
FP8X4 = mybir.dt.float8_e4m3fn_x4
FP4X4 = mybir.dt.float4_e2m1fn_x4
ALU = mybir.AluOpType
ACT = mybir.ActivationFunctionType

D, T, I, Q, E, K = 512, 2048, 512, 256, 512, 512
P = 128
PACK = 4
HALVES = Q // P
FLOPS = 2 * Q * I * (D + K + E)


def tile_attend_importanceread_pl_kernel(
    tc, query, query2, keys_words, keys_scales, keys2, l1, l2, size, vals, offs, out_0, out_1, out_2
):
    nc = tc.nc
    with ExitStack() as ctx:
        keep = ctx.enter_context(tc.tile_pool(name="keep", bufs=1))
        psum = ctx.enter_context(tc.psum_pool(name="psum", bufs=1))
        psum2 = ctx.enter_context(tc.psum_pool(name="psum2", bufs=2))

        def sb(name, shape, dtype, tag=None):
            return keep.tile(shape, dtype, name=name, tag=tag or name, align_bytes=64)

        def quantize(codes, scales, grouped):
            nc.vector.quantize_mx(out=codes.bitcast(FP8X4), scales=scales, in_=grouped)

        kscale_pool = sb("kscale_pool", [P, T], U8)
        nc.gpsimd.memset(kscale_pool[:].bitcast(I32), 0)

        keys2_planes = keys2.rearrange("(p t) n -> t p n", t=PACK)
        vals_planes = vals.rearrange("(p t) n -> t p n", t=PACK)
        k2_pool = [sb("k2_pool%d" % t, [P, T], F32) for t in range(PACK)]
        v_pool = [sb("v_pool%d" % t, [P, T], F32) for t in range(PACK)]
        offsets = keep.tile([P, I // 16], U16, name="offsets")
        rows = sb("rows", [P, I + P], F32)
        nc.vector.memset(rows[:], 0.0)
        kword_pool = sb("kword_pool", [P, T], U16)
        q_raw = sb("q_raw", [P, PACK, Q], F32)
        q2_raw = sb("q2_raw", [P, PACK, Q], F32)
        nc.sync.dma_start(k2_pool[0][:], keys2_planes[0])
        nc.sync.dma_start(offsets[:], offs)
        nc.sync.dma_start(k2_pool[1][:], keys2_planes[1])
        for g in range(4):
            nc.sync.dma_start(
                kscale_pool[g:P:32, :].bitcast(I32), keys_scales[0, g:16:4, :].bitcast(I32)
            )
        for t in range(2, PACK):
            nc.sync.dma_start(k2_pool[t][:], keys2_planes[t])
        nc.sync.dma_start(q2_raw[:], query2.rearrange("(p t) q -> p t q", t=PACK))
        nc.sync.dma_start(q_raw[:], query.rearrange("(p t) q -> p t q", t=PACK))
        nc.sync.dma_start(kword_pool[:].bitcast(I32), keys_words[0].bitcast(I32))
        for t in range(PACK):
            nc.sync.dma_start(v_pool[t][:], vals_planes[t])
        nc.gpsimd.dma_start(rows[0:HALVES, I:], l1.rearrange("(h p) o -> h (p o)", p=P))
        nc.gpsimd.dma_start(rows[HALVES : 2 * HALVES, I:], l2.rearrange("(h p) o -> h (p o)", p=P))
        nc.gpsimd.dma_start(rows[0:1, :I], size)

        ident = sb("ident", [P, P], F32)
        make_identity(nc, ident[:])

        size_t = psum.tile([P, PACK, P], F32, name="size_t", tag="acc0")
        for t in range(PACK):
            nc.tensor.transpose(size_t[:, t, :], rows[:, t:I:PACK], ident[:])
        size_sb = sb("size_sb", [P, PACK], F32)
        nc.scalar.copy(size_sb[:], size_t[:, :, 0])
        l_t = psum.tile([P, P], F32, name="l_t", tag="acc1")
        nc.tensor.transpose(l_t[:], rows[:, I:], ident[:])
        l_sb = sb("l_sb", [P, 2 * HALVES], F32)
        nc.scalar.copy(l_sb[:], l_t[:, : 2 * HALVES])

        k2_g = sb("k2_g", [P, 2, I], BF16)
        k2_grp = sb("k2_grp", [P, I, PACK], BF16)
        kscale = sb("kscale", [P, I], U8)
        kword = sb("kword", [P, I], U16)
        nc.vector.tensor_copy(k2_g[:, 0, :], k2_pool[0][:].indirect(offsets[:]))
        nc.vector.tensor_copy(k2_g[:, 1, :], k2_pool[1][:].indirect(offsets[:]))
        nc.vector.tensor_copy(kscale[:], kscale_pool[:].indirect(offsets[:]))
        nc.scalar.copy(k2_grp[:, :, 0:2], k2_g[:].rearrange("p t i -> p i t"))
        for t in range(2, PACK):
            nc.vector.tensor_copy(k2_grp[:, :, t], k2_pool[t][:].indirect(offsets[:]))
        bias = sb("bias", [P, HALVES], F32)
        nc.vector.tensor_tensor(bias[:], l_sb[:, HALVES:], l_sb[:, :HALVES], ALU.subtract)

        q_grp = sb("q_grp", [P, Q, PACK], BF16)
        q2_grp = sb("q2_grp", [P, Q, PACK], BF16)
        nc.scalar.activation(
            q2_grp[:].rearrange("p (c i) t -> p c t i", i=4),
            q2_raw[:].rearrange("p t (c i) -> p c t i", i=4),
            ACT.Copy,
            scale=-1.0,
        )
        nc.scalar.copy(
            q_grp[:].rearrange("p (c i) t -> p c t i", i=4), q_raw[:].rearrange("p t (c i) -> p c t i", i=4)
        )
        q_codes, q_scales = sb("q_codes", [P, Q], U32), sb("q_scales", [P, Q], U8)
        q2_codes, q2_scales = sb("q2_codes", [P, Q], U32), sb("q2_scales", [P, Q], U8)
        k2_codes, k2_scales = sb("k2_codes", [P, I], U32), sb("k2_scales", [P, I], U8)
        quantize(k2_codes[:], k2_scales[:], k2_grp[:].rearrange("p i t -> p (i t)"))
        quantize(q2_codes[:], q2_scales[:], q2_grp[:].rearrange("p q t -> p (q t)"))
        nc.vector.tensor_copy(kword[:], kword_pool[:].indirect(offsets[:]))
        quantize(q_codes[:], q_scales[:], q_grp[:].rearrange("p q t -> p (q t)"))

        ratio_t = []
        for h in range(HALVES):
            cols = slice(h * P, (h + 1) * P)
            score = psum.tile([P, I], F32, name="score%d" % h)
            nc.tensor.matmul_mx(
                out=score[:], lhsT=q2_codes[:, cols].bitcast(FP8X4), lhsT_scale=q2_scales[:, cols],
                rhs=k2_codes[:].bitcast(FP8X4), rhs_scale=k2_scales[:], start=True, stop=False,
            )
            nc.tensor.matmul_mx(
                out=score[:], lhsT=q_codes[:, cols].bitcast(FP8X4), lhsT_scale=q_scales[:, cols],
                rhs=kword[:].bitcast(FP4X4), rhs_scale=kscale[:], start=False, stop=True,
            )
            ratio = sb("ratio%d" % h, [P, PACK, P], F32)
            nc.scalar.activation(
                ratio[:], score[:].rearrange("p (s t) -> p t s", t=PACK), ACT.Exp, bias=bias[:, h : h + 1]
            )
            ratio_t.append(psum.tile([P, PACK, P], F32, name="ratio_t%d" % h))
            for t in range(PACK):
                nc.tensor.transpose(ratio_t[h][:, t, :], ratio[:, t, :], ident[:])

        out_rows = out_0.rearrange("(p t) q -> p t q", t=PACK)
        acc = [psum.tile([P, PACK, P], F32, name="acc%d" % h, tag="acc%d" % h) for h in range(HALVES)]
        o_grp = sb("o_grp", [P, Q, PACK], BF16)
        PLANE = P * PACK

        def turn(t):
            v_g = sb("v_g%d" % t, [P, I], BF16)
            nc.vector.tensor_copy(v_g[:], v_pool[t][:].indirect(offsets[:]))
            words = v_g[:].bitcast(F32)
            v_t = psum2.tile([P, 2, P], F32, name="v_t")
            for u in range(2):
                nc.tensor.transpose(v_t[:, u, :], words[:, u : 2 * P : 2], ident[:])
            return v_t

        def group(v_t, grouped):
            nc.scalar.copy(
                grouped.bitcast(F32).rearrange("p (e u) -> p e u", u=2), v_t[:].rearrange("p u e -> p e u")
            )

        def multiply(t, v_codes, v_scales):
            for h in range(HALVES):
                cols = slice(h * P, (h + 1) * P)
                nc.tensor.matmul_mx(
                    out=acc[h][:, t, :], lhsT=v_codes.bitcast(FP8X4), lhsT_scale=v_scales,
                    rhs=wv_codes[:, cols].bitcast(FP8X4), rhs_scale=wv_scales[:, cols], start=True, stop=True,
                )

        def store(t0, t1):
            o_sb = sb("o_sb%d" % t0, [P, t1 - t0, Q], F32)
            for h in reversed(range(HALVES)):
                nc.scalar.copy(o_sb[:, :, h * P : (h + 1) * P], acc[h][:, t0:t1, :])
            nc.sync.dma_start(out_rows[:, t0:t1, :], o_sb[:])

        v_t0 = turn(0)
        v_t1 = turn(1)
        wv_grp = sb("wv_grp", [P, Q * PACK + 2 * PLANE], BF16, "v_pool1")
        for h in range(HALVES):
            nc.vector.scalar_tensor_tensor(
                wv_grp[:, h * PLANE : (h + 1) * PLANE].rearrange("p (q t) -> p q t", t=PACK),
                ratio_t[h][:].rearrange("p t q -> p q t"),
                2.0,
                size_sb[:].unsqueeze(1).broadcast_to([P, P, PACK]),
                ALU.min,
                ALU.mult,
            )
        group(v_t0, wv_grp[:, 2 * PLANE : 3 * PLANE])
        group(v_t1, wv_grp[:, 3 * PLANE : 4 * PLANE])
        v_grp2 = sb("v_grp2", [P, PLANE], BF16)
        group(turn(2), v_grp2[:])
        wv_codes, wv_scales = sb("wv_codes", [P, 4 * P], U32, "v_pool2"), sb("wv_scales", [P, 4 * P], U8)
        quantize(wv_codes[:], wv_scales[:], wv_grp[:])
        for t in range(2):
            multiply(t, wv_codes[:, Q + t * P : Q + (t + 1) * P], wv_scales[:, Q + t * P : Q + (t + 1) * P])
        store(0, 2)
        v_grp3 = sb("v_grp3", [P, PLANE], BF16)
        group(turn(3), v_grp3[:])
        v_codes2, v_scales2 = sb("v_codes2", [P, P], U32, "v_pool3"), sb("v_scales2", [P, P], U8)
        quantize(v_codes2[:], v_scales2[:], v_grp2[:])
        multiply(2, v_codes2[:], v_scales2[:])
        store(2, 3)
        v_codes3, v_scales3 = sb("v_codes3", [P, P], U32), sb("v_scales3", [P, P], U8)
        quantize(v_codes3[:], v_scales3[:], v_grp3[:])
        multiply(3, v_codes3[:], v_scales3[:])
        nc.vector.tensor_copy(o_grp[:, 0:P, :], acc[0][:].rearrange("p t q -> p q t"))
        nc.scalar.copy(o_grp[:, P:Q, :], acc[1][:].rearrange("p t q -> p q t"))
        store(PACK - 1, PACK)

        o_codes, o_scales = sb("o_codes", [P, Q], U32), sb("o_scales", [P, Q], U8)
        quantize(o_codes[:], o_scales[:], o_grp[:].rearrange("p q t -> p (q t)"))
        nc.sync.dma_start(out_1[0].rearrange("p c r -> p (c r)").bitcast(I32), o_codes[:].bitcast(I32))
        for g in range(4):
            eng = nc.scalar if g % 2 == 0 else nc.sync
            eng.dma_start(
                out_2[0, g:16:4, :].bitcast(I32), o_scales[g:P:32, :].bitcast(I32)
            )
